import numpy as np
import ml_dtypes


def mxq(x, axis, fmt="e4m3"):
    dtype, down = {"e4m3": (ml_dtypes.float8_e4m3fn, 7), "e5m2": (ml_dtypes.float8_e5m2, 14)}[fmt]
    v = np.moveaxis(np.asarray(x, np.float32).astype(ml_dtypes.bfloat16).astype(np.float64), axis, -1)
    blocks = v.reshape(v.shape[:-1] + (-1, 32))
    amax = np.abs(blocks).max(-1, keepdims=True)
    byte = np.maximum(np.where(amax > 0, np.frexp(amax)[1] - 1 + 127, 0) - down, 1)
    scale = np.exp2(byte - 127.0)
    codes = (blocks / scale).astype(np.float32).astype(dtype).astype(np.float64)
    return np.moveaxis((codes * scale).reshape(v.shape), -1, axis)


WIDE = False


def mx_kscale(k):
    if not WIDE:
        return np.ones(k)
    levels = np.array([10, -10, 5, -5, 0])
    if k % 512:
        return np.exp2(np.random.permutation(np.resize(levels, k // 32))).repeat(32)
    a = np.empty((k // 512, 16))
    for p in range(k // 512):
        a[p, :8] = np.random.permutation(np.resize(levels, 8))
        for g in range(8):
            far = levels[np.abs(levels - a[p, g]) >= 10]
            a[p, g + 8] = far[np.random.randint(len(far))]
    return np.exp2(a.ravel()).repeat(32)


def f64(x):
    return np.asarray(x).astype(np.float64)


def striped(idx):
    return np.tile(np.asarray(idx).reshape(-1, 16).T, (8, 1)).astype(np.uint16)


def unstriped(offs):
    return offs[:16].T.reshape(-1).astype(np.int64)


E2M1 = np.array([0.0, 0.5, 1.0, 1.5, 2.0, 3.0, 4.0, 6.0, -0.0, -0.5, -1.0, -1.5, -2.0, -3.0, -4.0, -6.0])


def pack_weight(w, fmt):
    k, n = w.shape
    w = f64(np.asarray(w, np.float32).astype(ml_dtypes.bfloat16)).reshape(k // 32, 32, n)
    amax = np.abs(w).max(1)
    if fmt == "e4m3":
        byte = np.frexp(amax)[1] - 1 + 127 - 7
    else:
        mant, ex = np.frexp(amax / 6.0)
        byte = np.where(mant > 0.5, ex, ex - 1) + 127
    byte = np.clip(np.where(amax > 0, byte, 1), 1, 254)
    scaled = (w * np.exp2(127.0 - byte)[:, None, :]).reshape(k, n).astype(np.float32)
    by_word = np.ascontiguousarray(scaled.reshape(k // 512, 128, 4, n).transpose(0, 1, 3, 2))
    if fmt == "e4m3":
        words = by_word.astype(ml_dtypes.float8_e4m3fn).view(np.uint8)
    else:
        c = by_word.astype(ml_dtypes.float4_e2m1fn).view(np.uint8) & 0xF
        words = (c[..., 0::2] | (c[..., 1::2] << 4)).reshape(k // 512, 128, 2 * n)
    return np.ascontiguousarray(words), np.ascontiguousarray(byte.astype(np.uint8).reshape(k // 512, 16, n))


def unpack_weight(words, scales, fmt):
    g, _, n = scales.shape
    words = np.ascontiguousarray(words).reshape(g, 128, n, -1)
    if fmt == "e4m3":
        vals = words.view(ml_dtypes.float8_e4m3fn).astype(np.float64)
    else:
        nib = np.empty((g, 128, n, 4), np.uint8)
        nib[..., 0::2] = words & 0xF
        nib[..., 1::2] = words >> 4
        vals = E2M1[nib]
    vals = vals * np.repeat(np.exp2(scales.astype(np.float64) - 127.0), 8, axis=1)[..., None]
    return vals.transpose(0, 1, 3, 2).reshape(g * 512, n)


D, E, T, I, Q = 512, 512, 2048, 512, 128


def setup_inputs():
    n = np.random.standard_normal
    idx = np.random.permutation(T)[:I]
    fd = mx_kscale(D)
    fi = mx_kscale(I)
    ti = np.ones(T)
    ti[idx] = fi
    keysp = pack_weight(n((D, T)) / fd[:, None], "e2m1")
    return {
        "query": (n((D, Q)) * 1.0 / np.sqrt(D) * fd[:, None]).astype(np.float32),
        "keys_words": keysp[0],
        "keys_scales": keysp[1],
        "sharp": (np.random.uniform(0.4, 1.0, (Q, 1))).astype(np.float32),
        "dquery": (n((D, Q)) * 0.6 / np.sqrt(D) * fd[:, None]).astype(np.float32),
        "os": (np.random.uniform(4.0, 16.0, (1, I)) * fi).astype(np.float32),
        "vals": (n((E, T)) / ti).astype(np.float32),
        "offs": striped(idx),
    }


def reference(query, keys_words, keys_scales, sharp, dquery, os, vals, offs):
    idx = unstriped(offs)
    keysu = unpack_weight(keys_words, keys_scales, "e2m1")
    queryq = mxq(f64(query), 0, "e4m3")
    keysidxg = keysu[:, idx]
    a = queryq.T @ keysidxg
    dqueryq = mxq(f64(dquery), 0, "e4m3")
    ta = dqueryq.T @ keysidxg
    m1 = np.mean(a, axis=1, keepdims=True)
    ce = a - m1
    sd = np.sqrt(np.mean(np.square(ce), axis=1, keepdims=True) + 0.05)
    s = ce / sd * f64(sharp)
    p = np.exp(s - np.max(s, axis=1, keepdims=True))
    z = np.sum(p, axis=1, keepdims=True)
    tm1 = np.mean(ta, axis=1, keepdims=True)
    tce = ta - tm1
    tsd = np.mean(tce * ce * 2.0, axis=1, keepdims=True) * 0.5 / sd
    ts = (tce - tsd * ce / sd) / sd * f64(sharp)
    tp = ts * p
    tz = np.sum(tp, axis=1, keepdims=True)
    tw = (tp - tz * p / z) / z
    wo1 = tw * f64(os)
    wt1 = wo1.T
    vt1 = f64(vals)[:, idx].T
    wt1q = mxq(wt1, 0, "e4m3")
    vt1q = mxq(vt1, 0, "e4m3")
    o = wt1q.T @ vt1q
    return o

@@ -1,0 +1,196 @@
+from contextlib import ExitStack
+
+import concourse.mybir as mybir
+from concourse.masks import make_identity
+
+F32 = mybir.dt.float32
+BF16 = mybir.dt.bfloat16
+I32 = mybir.dt.int32
+U32 = mybir.dt.uint32
+U16 = mybir.dt.uint16
+U8 = mybir.dt.uint8
+FP8X4 = mybir.dt.float8_e4m3fn_x4
+FP4X4 = mybir.dt.float4_e2m1fn_x4
+ALU = mybir.AluOpType
+ACT = mybir.ActivationFunctionType
+
+D, E, T, I, Q = 512, 512, 2048, 512, 128
+P = 128
+PACK = 4
+EPS = 0.05
+FLOPS = 2 * Q * I * (2 * D + E)
+
+
+def tile_attend_ttstandardised_kernel(tc, query, keys_words, keys_scales, sharp, dquery, slot_factor, vals, offs, out):
+    nc = tc.nc
+    with ExitStack() as ctx:
+        sb = ctx.enter_context(tc.tile_pool(name="sb", bufs=1))
+        ps = ctx.enter_context(tc.psum_pool(name="ps", bufs=1))
+        ps2 = ctx.enter_context(tc.psum_pool(name="ps2", bufs=2))
+
+        offsets = sb.tile([P, I // 16], U16, name="offsets")
+        nc.sync.dma_start(offsets[:], offs)
+
+        key_bytes = sb.tile([P, T], U8, name="key_bytes")
+        nc.vector.memset(key_bytes[:].bitcast(I32), 0)
+        for quad in range(4):
+            nc.sync.dma_start(
+                key_bytes[32 * quad : 32 * quad + 4, :].bitcast(I32),
+                keys_scales[0, 4 * quad : 4 * quad + 4, :].bitcast(I32),
+            )
+        key_words = sb.tile([P, T], U16, name="key_words")
+        nc.sync.dma_start(key_words[:].bitcast(I32), keys_words[0].bitcast(I32))
+
+        raw = []
+        for name, src in (("q_raw", query), ("dq_raw", dquery)):
+            t = sb.tile([P, PACK, Q], F32, name=name)
+            nc.sync.dma_start(t[:], src.rearrange("(p j) q -> p j q", j=PACK))
+            raw.append(t)
+        val_rows = []
+        for j in range(E // P):
+            t = sb.tile([P, T], F32, name="val_rows%d" % j)
+            nc.sync.dma_start(t[:], vals[j * P : (j + 1) * P, :])
+            val_rows.append(t)
+
+        sharp_col = sb.tile([P, 1], F32, name="sharp_col")
+        nc.gpsimd.dma_start(sharp_col[:], sharp)
+        os_cols = sb.tile([P, PACK], F32, name="os_cols")
+        nc.gpsimd.dma_start(os_cols[:], slot_factor.rearrange("o (p t) -> (o p) t", t=PACK))
+
+        ones = sb.tile([P, 1], F32, name="ones")
+        nc.gpsimd.memset(ones[:], 1.0)
+        minus_half = sb.tile([P, 1], F32, name="minus_half")
+        nc.scalar.activation(minus_half[:], ones[:], ACT.Copy, scale=-0.5)
+        ident = sb.tile([P, P], F32, name="ident")
+        make_identity(nc, ident[:])
+
+        by_r = sb.tile([P, 3], F32, name="by_r")
+        nc.vector.memset(by_r[:, 2:3], -1.0 / I)
+
+        picked_bytes = sb.tile([P, I], U8, name="picked_bytes", align_bytes=64)
+        nc.vector.tensor_copy(picked_bytes[:], key_bytes[:].indirect(offsets[:]))
+        picked_words = sb.tile([P, I], U16, name="picked_words", align_bytes=64)
+        nc.vector.tensor_copy(picked_words[:], key_words[:].indirect(offsets[:]))
+
+        os_ps = ps.tile([P, PACK, P], F32, name="os_ps")
+        for t in range(PACK):
+            nc.tensor.transpose(os_ps[:, t, :], os_cols[:, t : t + 1].to_broadcast([P, P]), ident[:])
+
+        scores = []
+        for name, src in zip(("q", "dq"), raw):
+            grouped = sb.tile([P, Q, PACK], BF16, name=name + "_grouped", align_bytes=64)
+            nc.scalar.activation(grouped[:], src[:].rearrange("p j q -> p q j"), ACT.Copy)
+            codes = sb.tile([P, Q], U32, name=name + "_codes", align_bytes=64)
+            scales = sb.tile([P, Q], U8, name=name + "_scales", align_bytes=64)
+            nc.vector.quantize_mx(
+                out=codes[:].bitcast(FP8X4), scales=scales[:], in_=grouped[:].rearrange("p q j -> p (q j)")
+            )
+            bank = ps.tile([Q, I], F32, name=name + "_bank")
+            nc.tensor.matmul_mx(
+                out=bank[:],
+                lhsT=codes[:].bitcast(FP8X4),
+                lhsT_scale=scales[:],
+                rhs=picked_words[:].bitcast(FP4X4),
+                rhs_scale=picked_bytes[:],
+                start=True,
+                stop=True,
+            )
+            scores.append(bank)
+        a_ps, ta_ps = scores
+
+        neg_sharp = sb.tile([P, 1], F32, name="neg_sharp")
+        nc.scalar.activation(neg_sharp[:], sharp_col[:], ACT.Copy, scale=-1.0)
+        nc.scalar.activation(by_r[:, 0:1], sharp_col[:], ACT.Copy)
+
+        def col(name):
+            return sb.tile([P, 1], F32, name=name)
+
+        def turn_and_quantise(name, rows):
+            words = rows[:].bitcast(F32)
+            turned = ps2.tile([P, 2, P], F32, name="turned")
+            for u in range(2):
+                nc.tensor.transpose(turned[:, u, :], words[:, u::2], ident[:])
+            grouped = sb.tile([P, P * PACK], BF16, name=name + "_grouped", align_bytes=64)
+            nc.scalar.copy(
+                grouped[:].bitcast(F32).rearrange("p (x u) -> p x u", u=2), turned[:].rearrange("p u x -> p x u")
+            )
+            codes = sb.tile([P, P], U32, name=name + "_codes", align_bytes=64)
+            scales = sb.tile([P, P], U8, name=name + "_scales", align_bytes=64)
+            nc.vector.quantize_mx(out=codes[:].bitcast(FP8X4), scales=scales[:], in_=grouped[:])
+            return codes, scales
+
+        def gather_values(j):
+            picked = sb.tile([P, I], BF16, name="picked_vals%d" % j)
+            nc.vector.tensor_copy(picked[:], val_rows[j][:].indirect(offsets[:]))
+            return turn_and_quantise("v%d" % j, picked)
+
+        a_sb = sb.tile([Q, I], F32, name="a_sb")
+        sum_a = col("sum_a")
+        nc.scalar.activation(a_sb[:], a_ps[:], ACT.Identity, accum_out=sum_a[:])
+        neg_mean = col("neg_mean")
+        nc.scalar.activation(neg_mean[:], sum_a[:], ACT.Copy, scale=-1.0 / I)
+        junk_s = sb.tile([Q, I], BF16, name="junk_s")
+        sum_sq = col("sum_sq")
+        nc.scalar.activation(junk_s[:], a_ps[:], ACT.Square, bias=neg_mean[:], accum_out=sum_sq[:])
+        var_eps = col("var_eps")
+        nc.scalar.activation(var_eps[:], sum_sq[:], ACT.Copy, scale=1.0 / I, bias=EPS)
+        r = col("r")
+        nc.gpsimd.tensor_tensor(r[:], var_eps[:], minus_half[:], ALU.pow)
+
+        junk_v = sb.tile([Q, I], BF16, name="junk_v")
+        nc.vector.tensor_scalar(junk_v[:], a_sb[:], neg_sharp[:], None, ALU.mult, ALU.min, accum_out=by_r[:, 1:2])
+        cov = col("cov")
+        junk_c = sb.tile([Q, I], BF16, name="junk_c")
+        nc.vector.scalar_tensor_tensor(junk_c[:], a_sb[:], neg_mean[:], ta_ps[:], ALU.add, ALU.mult, accum_out=cov[:])
+
+        times_r = sb.tile([P, 3], F32, name="times_r")
+        nc.scalar.activation(times_r[:], by_r[:], ACT.Copy, scale=r[:])
+        p = sb.tile([Q, I], F32, name="p")
+        z = col("z")
+        nc.scalar.activation(p[:], a_ps[:], ACT.Exp, scale=times_r[:, 0:1], bias=times_r[:, 1:2], accum_out=z[:])
+
+        vq = [gather_values(0)]
+
+        neg_slope = col("neg_slope")
+        nc.vector.tensor_scalar(neg_slope[:], cov[:], r[:], times_r[:, 2:3], ALU.mult, ALU.mult)
+        u = sb.tile([Q, I], F32, name="u")
+        nc.vector.scalar_tensor_tensor(u[:], a_sb[:], neg_slope[:], ta_ps[:], ALU.mult, ALU.add)
+        rz = col("rz")
+        nc.vector.reciprocal(rz[:], z[:])
+        cz = col("cz")
+        nc.scalar.activation(cz[:], times_r[:, 0:1], ACT.Copy, scale=rz[:])
+        u_mean = col("u_mean")
+        junk_u = sb.tile([Q, I], BF16, name="junk_u")
+        nc.vector.scalar_tensor_tensor(junk_u[:], u[:], rz[:], p[:], ALU.mult, ALU.mult, accum_out=u_mean[:])
+        x = sb.tile([Q, I], F32, name="x")
+        nc.vector.scalar_tensor_tensor(
+            x[:].rearrange("q (p t) -> q p t", t=PACK),
+            p[:].rearrange("q (p t) -> q p t", t=PACK),
+            cz[:],
+            os_ps[:].rearrange("q t p -> q p t"),
+            ALU.mult,
+            ALU.mult,
+        )
+        w = sb.tile([Q, I], BF16, name="w")
+        nc.vector.scalar_tensor_tensor(w[:], u[:], u_mean[:], x[:], ALU.subtract, ALU.mult)
+        w_codes, w_scales = turn_and_quantise("w", w)
+
+        for j in range(1, E // P):
+            vq.append(gather_values(j))
+
+        for lo, hi in ((0, 3), (3, 4)):
+            bank = ps.tile([Q, (hi - lo) * P], F32, name="out_bank%d" % lo)
+            for j in range(lo, hi):
+                codes, scales = vq[j]
+                nc.tensor.matmul_mx(
+                    out=bank[:, (j - lo) * P : (j - lo + 1) * P],
+                    lhsT=w_codes[:].bitcast(FP8X4),
+                    lhsT_scale=w_scales[:],
+                    rhs=codes[:].bitcast(FP8X4),
+                    rhs_scale=scales[:],
+                    start=True,
+                    stop=True,
+                )
+            result = sb.tile([Q, (hi - lo) * P], F32, name="result%d" % lo)
+            nc.scalar.copy(result[:], bank[:])
+            nc.sync.dma_start(out[:, lo * P : hi * P], result[:])

@@ -26,10 +26,11 @@ def tile_attend_ttstandardised_kernel(tc, query, keys_words, keys_scales, sharp,
     with ExitStack() as ctx:
         sb = ctx.enter_context(tc.tile_pool(name="sb", bufs=1))
         ps = ctx.enter_context(tc.psum_pool(name="ps", bufs=1))
-        ps2 = ctx.enter_context(tc.psum_pool(name="ps2", bufs=2))
 
         offsets = sb.tile([P, I // 16], U16, name="offsets")
         nc.sync.dma_start(offsets[:], offs)
+
+        raw = [sb.tile([P, PACK, Q], F32, name=name, tag=name) for name in ("q_raw", "dq_raw")]
 
         key_bytes = sb.tile([P, T], U8, name="key_bytes")
         nc.vector.memset(key_bytes[:].bitcast(I32), 0)
@@ -41,19 +42,15 @@ def tile_attend_ttstandardised_kernel(tc, query, keys_words, keys_scales, sharp,
         key_words = sb.tile([P, T], U16, name="key_words")
         nc.sync.dma_start(key_words[:].bitcast(I32), keys_words[0].bitcast(I32))
 
-        raw = []
-        for name, src in (("q_raw", query), ("dq_raw", dquery)):
-            t = sb.tile([P, PACK, Q], F32, name=name)
-            nc.sync.dma_start(t[:], src.rearrange("(p j) q -> p j q", j=PACK))
-            raw.append(t)
-        val_rows = []
+        val_rows = [sb.tile([P, T], F32, name="val_rows%d" % j, tag="val_rows%d" % j, align_bytes=64) for j in range(E // P)]
+        nc.sync.dma_start(raw[0][:], query.rearrange("(p j) q -> p j q", j=PACK))
+        nc.sync.dma_start(raw[1][:], dquery.rearrange("(p j) q -> p j q", j=PACK))
         for j in range(E // P):
-            t = sb.tile([P, T], F32, name="val_rows%d" % j)
-            nc.sync.dma_start(t[:], vals[j * P : (j + 1) * P, :])
-            val_rows.append(t)
+            nc.sync.dma_start(val_rows[j][:], vals[j * P : (j + 1) * P, :])
 
         sharp_col = sb.tile([P, 1], F32, name="sharp_col")
         nc.gpsimd.dma_start(sharp_col[:], sharp)
+
         os_cols = sb.tile([P, PACK], F32, name="os_cols")
         nc.gpsimd.dma_start(os_cols[:], slot_factor.rearrange("o (p t) -> (o p) t", t=PACK))
 
@@ -64,17 +61,11 @@ def tile_attend_ttstandardised_kernel(tc, query, keys_words, keys_scales, sharp,
         ident = sb.tile([P, P], F32, name="ident")
         make_identity(nc, ident[:])
 
-        by_r = sb.tile([P, 3], F32, name="by_r")
-        nc.vector.memset(by_r[:, 2:3], -1.0 / I)
 
         picked_bytes = sb.tile([P, I], U8, name="picked_bytes", align_bytes=64)
         nc.vector.tensor_copy(picked_bytes[:], key_bytes[:].indirect(offsets[:]))
         picked_words = sb.tile([P, I], U16, name="picked_words", align_bytes=64)
         nc.vector.tensor_copy(picked_words[:], key_words[:].indirect(offsets[:]))
-
-        os_ps = ps.tile([P, PACK, P], F32, name="os_ps")
-        for t in range(PACK):
-            nc.tensor.transpose(os_ps[:, t, :], os_cols[:, t : t + 1].to_broadcast([P, P]), ident[:])
 
         scores = []
         for name, src in zip(("q", "dq"), raw):
@@ -85,7 +76,7 @@ def tile_attend_ttstandardised_kernel(tc, query, keys_words, keys_scales, sharp,
             nc.vector.quantize_mx(
                 out=codes[:].bitcast(FP8X4), scales=scales[:], in_=grouped[:].rearrange("p q j -> p (q j)")
             )
-            bank = ps.tile([Q, I], F32, name=name + "_bank")
+            bank = ps.tile([Q, I], F32, name=name + "_bank", tag=name + "_bank")
             nc.tensor.matmul_mx(
                 out=bank[:],
                 lhsT=codes[:].bitcast(FP8X4),
@@ -98,37 +89,41 @@ def tile_attend_ttstandardised_kernel(tc, query, keys_words, keys_scales, sharp,
             scores.append(bank)
         a_ps, ta_ps = scores
 
-        neg_sharp = sb.tile([P, 1], F32, name="neg_sharp")
-        nc.scalar.activation(neg_sharp[:], sharp_col[:], ACT.Copy, scale=-1.0)
+        os_ps = ps.tile([P, PACK, P], F32, name="os_ps", tag="os_ps")
+        for t in range(PACK):
+            nc.tensor.transpose(os_ps[:, t, :], os_cols[:, t : t + 1].to_broadcast([P, P]), ident[:])
+
+        by_r = sb.tile([P, 5], F32, name="by_r", tag="dq_raw")
+        nc.scalar.activation(by_r[:, 2:3], sharp_col[:], ACT.Copy, scale=-1.0)
         nc.scalar.activation(by_r[:, 0:1], sharp_col[:], ACT.Copy)
+        nc.scalar.activation(by_r[:, 3:4], ones[:], ACT.Copy, scale=float(I))
 
         def col(name):
             return sb.tile([P, 1], F32, name=name)
 
-        def turn_and_quantise(name, rows):
-            words = rows[:].bitcast(F32)
-            turned = ps2.tile([P, 2, P], F32, name="turned")
-            for u in range(2):
-                nc.tensor.transpose(turned[:, u, :], words[:, u::2], ident[:])
-            grouped = sb.tile([P, P * PACK], BF16, name=name + "_grouped", align_bytes=64)
+        def turn(rows, bank, grouped):
+            for n, tile in enumerate(rows):
+                words = tile[:].bitcast(F32)
+                for u in range(2):
+                    nc.tensor.transpose(bank[:, n, u, :], words[:, u::2], ident[:])
             nc.scalar.copy(
-                grouped[:].bitcast(F32).rearrange("p (x u) -> p x u", u=2), turned[:].rearrange("p u x -> p x u")
+                grouped.bitcast(F32).rearrange("p (n x u) -> p n x u", n=len(rows), u=2),
+                bank[:].rearrange("p n u x -> p n x u"),
             )
-            codes = sb.tile([P, P], U32, name=name + "_codes", align_bytes=64)
-            scales = sb.tile([P, P], U8, name=name + "_scales", align_bytes=64)
-            nc.vector.quantize_mx(out=codes[:].bitcast(FP8X4), scales=scales[:], in_=grouped[:])
-            return codes, scales
 
         def gather_values(j):
             picked = sb.tile([P, I], BF16, name="picked_vals%d" % j)
             nc.vector.tensor_copy(picked[:], val_rows[j][:].indirect(offsets[:]))
-            return turn_and_quantise("v%d" % j, picked)
+            return picked
 
+        junk_v = sb.tile([Q, I], BF16, name="junk_v")
+        nc.vector.tensor_scalar(junk_v[:], a_ps[:], by_r[:, 2:3], None, ALU.mult, ALU.min, accum_out=by_r[:, 1:2])
+        picked = [gather_values(0)]
         a_sb = sb.tile([Q, I], F32, name="a_sb")
-        sum_a = col("sum_a")
-        nc.scalar.activation(a_sb[:], a_ps[:], ACT.Identity, accum_out=sum_a[:])
         neg_mean = col("neg_mean")
-        nc.scalar.activation(neg_mean[:], sum_a[:], ACT.Copy, scale=-1.0 / I)
+        nc.scalar.activation(a_sb[:], a_ps[:], ACT.Identity, scale=-1.0 / I, accum_out=neg_mean[:])
+        mean_n = col("mean_n")
+        nc.scalar.activation(mean_n[:], neg_mean[:], ACT.Copy, scale=1.0 / I)
         junk_s = sb.tile([Q, I], BF16, name="junk_s")
         sum_sq = col("sum_sq")
         nc.scalar.activation(junk_s[:], a_ps[:], ACT.Square, bias=neg_mean[:], accum_out=sum_sq[:])
@@ -137,31 +132,31 @@ def tile_attend_ttstandardised_kernel(tc, query, keys_words, keys_scales, sharp,
         r = col("r")
         nc.gpsimd.tensor_tensor(r[:], var_eps[:], minus_half[:], ALU.pow)
 
-        junk_v = sb.tile([Q, I], BF16, name="junk_v")
-        nc.vector.tensor_scalar(junk_v[:], a_sb[:], neg_sharp[:], None, ALU.mult, ALU.min, accum_out=by_r[:, 1:2])
-        cov = col("cov")
         junk_c = sb.tile([Q, I], BF16, name="junk_c")
-        nc.vector.scalar_tensor_tensor(junk_c[:], a_sb[:], neg_mean[:], ta_ps[:], ALU.add, ALU.mult, accum_out=cov[:])
+        nc.vector.scalar_tensor_tensor(
+            junk_c[:], a_sb[:], mean_n[:], ta_ps[:], ALU.subtract, ALU.mult, accum_out=by_r[:, 4:5]
+        )
+        picked.append(gather_values(1))
 
-        times_r = sb.tile([P, 3], F32, name="times_r")
+        times_r = sb.tile([P, 5], F32, name="times_r")
         nc.scalar.activation(times_r[:], by_r[:], ACT.Copy, scale=r[:])
+        slope = col("slope")
+        nc.scalar.activation(slope[:], times_r[:, 4:5], ACT.Copy, scale=times_r[:, 3:4])
         p = sb.tile([Q, I], F32, name="p")
         z = col("z")
         nc.scalar.activation(p[:], a_ps[:], ACT.Exp, scale=times_r[:, 0:1], bias=times_r[:, 1:2], accum_out=z[:])
 
-        vq = [gather_values(0)]
-
-        neg_slope = col("neg_slope")
-        nc.vector.tensor_scalar(neg_slope[:], cov[:], r[:], times_r[:, 2:3], ALU.mult, ALU.mult)
-        u = sb.tile([Q, I], F32, name="u")
-        nc.vector.scalar_tensor_tensor(u[:], a_sb[:], neg_slope[:], ta_ps[:], ALU.mult, ALU.add)
+        u = sb.tile([Q, I], F32, name="u", tag="val_rows1", align_bytes=64)
+        nc.vector.scalar_tensor_tensor(u[:], a_sb[:], slope[:], ta_ps[:], ALU.mult, ALU.subtract)
         rz = col("rz")
         nc.vector.reciprocal(rz[:], z[:])
         cz = col("cz")
-        nc.scalar.activation(cz[:], times_r[:, 0:1], ACT.Copy, scale=rz[:])
-        u_mean = col("u_mean")
+        nc.scalar.activation(cz[:], times_r[:, 2:3], ACT.Copy, scale=rz[:])
+        u_sum = col("u_sum")
         junk_u = sb.tile([Q, I], BF16, name="junk_u")
-        nc.vector.scalar_tensor_tensor(junk_u[:], u[:], rz[:], p[:], ALU.mult, ALU.mult, accum_out=u_mean[:])
+        nc.vector.scalar_tensor_tensor(junk_u[:], u[:], 1.0, p[:], ALU.mult, ALU.mult, accum_out=u_sum[:])
+        u_mean = col("u_mean")
+        nc.scalar.activation(u_mean[:], u_sum[:], ACT.Copy, scale=rz[:])
         x = sb.tile([Q, I], F32, name="x")
         nc.vector.scalar_tensor_tensor(
             x[:].rearrange("q (p t) -> q p t", t=PACK),
@@ -173,24 +168,42 @@ def tile_attend_ttstandardised_kernel(tc, query, keys_words, keys_scales, sharp,
         )
         w = sb.tile([Q, I], BF16, name="w")
         nc.vector.scalar_tensor_tensor(w[:], u[:], u_mean[:], x[:], ALU.subtract, ALU.mult)
-        w_codes, w_scales = turn_and_quantise("w", w)
+        picked.append(gather_values(2))
+        picked.append(gather_values(3))
 
-        for j in range(1, E // P):
-            vq.append(gather_values(j))
+        grouped = sb.tile([P, 5 * I], BF16, name="grouped", align_bytes=64)
+        turn(picked[0:2], ps.tile([P, 2, 2, P], F32, name="turned01", tag="q_bank"), grouped[:, 0 : 2 * I])
+        turn([w], ps.tile([P, 1, 2, P], F32, name="turned_w"), grouped[:, 4 * I :])
+        turn(picked[2:3], ps.tile([P, 1, 2, P], F32, name="turned2"), grouped[:, 2 * I : 3 * I])
+        turn(picked[3:4], ps.tile([P, 1, 2, P], F32, name="turned3"), grouped[:, 3 * I : 4 * I])
 
-        for lo, hi in ((0, 3), (3, 4)):
-            bank = ps.tile([Q, (hi - lo) * P], F32, name="out_bank%d" % lo)
-            for j in range(lo, hi):
-                codes, scales = vq[j]
-                nc.tensor.matmul_mx(
-                    out=bank[:, (j - lo) * P : (j - lo + 1) * P],
-                    lhsT=w_codes[:].bitcast(FP8X4),
-                    lhsT_scale=w_scales[:],
-                    rhs=codes[:].bitcast(FP8X4),
-                    rhs_scale=scales[:],
-                    start=True,
-                    stop=True,
-                )
-            result = sb.tile([Q, (hi - lo) * P], F32, name="result%d" % lo)
-            nc.scalar.copy(result[:], bank[:])
-            nc.sync.dma_start(out[:, lo * P : hi * P], result[:])
+        codes = sb.tile([P, 5 * P], U32, name="codes", tag="val_rows3", align_bytes=64)
+        scales = sb.tile([P, 5 * P], U8, name="scales", align_bytes=64)
+        for lo, hi in ((4, 5), (0, 2), (2, 3), (3, 4)):
+            nc.vector.quantize_mx(
+                out=codes[:, lo * P : hi * P].bitcast(FP8X4),
+                scales=scales[:, lo * P : hi * P],
+                in_=grouped[:, lo * I : hi * I],
+            )
+
+        def product(bank, lo, hi):
+            nc.tensor.matmul_mx(
+                out=bank,
+                lhsT=codes[:, 4 * P :].bitcast(FP8X4),
+                lhsT_scale=scales[:, 4 * P :],
+                rhs=codes[:, lo:hi].bitcast(FP8X4),
+                rhs_scale=scales[:, lo:hi],
+                start=True,
+                stop=True,
+            )
+
+        for lo, hi, tag, copy in (
+            (0, 2 * P, "out01", nc.scalar.copy),
+            (2 * P, 3 * P, "os_ps", nc.vector.tensor_copy),
+            (3 * P, 4 * P, "out3", nc.vector.tensor_copy),
+        ):
+            bank = ps.tile([Q, hi - lo], F32, name="out_bank%d" % lo, tag=tag)
+            product(bank[:], lo, hi)
+            result = sb.tile([Q, hi - lo], F32, name="result%d" % lo)
+            copy(result[:], bank[:])
+            nc.sync.dma_start(out[:, lo:hi], result[:])

@@ -17,8 +17,15 @@ ACT = mybir.ActivationFunctionType
 D, E, T, I, Q = 512, 512, 2048, 512, 128
 P = 128
 PACK = 4
+LIST_ROWS = 16
+QUADRANT = 32
+VALUE_TILES = E // P
+MX_ALIGN = 64
 EPS = 0.05
 FLOPS = 2 * Q * I * (2 * D + E)
+
+SHARP, NEG_MAX, NEG_SHARP, SLOTS, NEG_COV = range(5)
+WEIGHTS = VALUE_TILES
 
 
 def tile_attend_ttstandardised_kernel(tc, query, keys_words, keys_scales, sharp, dquery, slot_factor, vals, offs, out):
@@ -27,183 +34,188 @@ def tile_attend_ttstandardised_kernel(tc, query, keys_words, keys_scales, sharp,
         sb = ctx.enter_context(tc.tile_pool(name="sb", bufs=1))
         ps = ctx.enter_context(tc.psum_pool(name="ps", bufs=1))
 
-        offsets = sb.tile([P, I // 16], U16, name="offsets")
+        def column(name):
+            return sb.tile([P, 1], F32, name=name)
+
+        def one(tile, n):
+            return tile[:, n : n + 1]
+
+        offsets = sb.tile([P, I // LIST_ROWS], U16, name="offsets")
         nc.sync.dma_start(offsets[:], offs)
 
         raw = [sb.tile([P, PACK, Q], F32, name=name, tag=name) for name in ("q_raw", "dq_raw")]
 
         key_bytes = sb.tile([P, T], U8, name="key_bytes")
         nc.vector.memset(key_bytes[:].bitcast(I32), 0)
-        for quad in range(4):
+        for quad in range(P // QUADRANT):
             nc.sync.dma_start(
-                key_bytes[32 * quad : 32 * quad + 4, :].bitcast(I32),
+                key_bytes[QUADRANT * quad : QUADRANT * quad + 4, :].bitcast(I32),
                 keys_scales[0, 4 * quad : 4 * quad + 4, :].bitcast(I32),
             )
         key_words = sb.tile([P, T], U16, name="key_words")
         nc.sync.dma_start(key_words[:].bitcast(I32), keys_words[0].bitcast(I32))
 
-        val_rows = [sb.tile([P, T], F32, name="val_rows%d" % j, tag="val_rows%d" % j, align_bytes=64) for j in range(E // P)]
-        nc.sync.dma_start(raw[0][:], query.rearrange("(p j) q -> p j q", j=PACK))
-        nc.sync.dma_start(raw[1][:], dquery.rearrange("(p j) q -> p j q", j=PACK))
-        for j in range(E // P):
+        val_rows = [
+            sb.tile([P, T], F32, name="val_rows%d" % j, tag="val_rows%d" % j, align_bytes=MX_ALIGN)
+            for j in range(VALUE_TILES)
+        ]
+        nc.sync.dma_start(raw[0][:], query.rearrange("(p t) q -> p t q", t=PACK))
+        nc.sync.dma_start(raw[1][:], dquery.rearrange("(p t) q -> p t q", t=PACK))
+        for j in range(VALUE_TILES):
             nc.sync.dma_start(val_rows[j][:], vals[j * P : (j + 1) * P, :])
 
-        sharp_col = sb.tile([P, 1], F32, name="sharp_col")
+        sharp_col = column("sharp_col")
         nc.gpsimd.dma_start(sharp_col[:], sharp)
-
         os_cols = sb.tile([P, PACK], F32, name="os_cols")
         nc.gpsimd.dma_start(os_cols[:], slot_factor.rearrange("o (p t) -> (o p) t", t=PACK))
 
-        ones = sb.tile([P, 1], F32, name="ones")
+        ones = column("ones")
         nc.gpsimd.memset(ones[:], 1.0)
-        minus_half = sb.tile([P, 1], F32, name="minus_half")
+        minus_half = column("minus_half")
         nc.scalar.activation(minus_half[:], ones[:], ACT.Copy, scale=-0.5)
         ident = sb.tile([P, P], F32, name="ident")
         make_identity(nc, ident[:])
 
-
-        picked_bytes = sb.tile([P, I], U8, name="picked_bytes", align_bytes=64)
+        picked_bytes = sb.tile([P, I], U8, name="picked_bytes", align_bytes=MX_ALIGN)
         nc.vector.tensor_copy(picked_bytes[:], key_bytes[:].indirect(offsets[:]))
-        picked_words = sb.tile([P, I], U16, name="picked_words", align_bytes=64)
+        picked_words = sb.tile([P, I], U16, name="picked_words", align_bytes=MX_ALIGN)
         nc.vector.tensor_copy(picked_words[:], key_words[:].indirect(offsets[:]))
 
         scores = []
-        for name, src in zip(("q", "dq"), raw):
-            grouped = sb.tile([P, Q, PACK], BF16, name=name + "_grouped", align_bytes=64)
-            nc.scalar.activation(grouped[:], src[:].rearrange("p j q -> p q j"), ACT.Copy)
-            codes = sb.tile([P, Q], U32, name=name + "_codes", align_bytes=64)
-            scales = sb.tile([P, Q], U8, name=name + "_scales", align_bytes=64)
+        for name, rows in zip(("q", "dq"), raw):
+            q_grouped = sb.tile([P, Q, PACK], BF16, name=name + "_grouped", align_bytes=MX_ALIGN)
+            nc.scalar.activation(q_grouped[:], rows[:].rearrange("p t q -> p q t"), ACT.Copy)
+            q_codes = sb.tile([P, Q], U32, name=name + "_codes", align_bytes=MX_ALIGN)
+            q_scales = sb.tile([P, Q], U8, name=name + "_scales", align_bytes=MX_ALIGN)
             nc.vector.quantize_mx(
-                out=codes[:].bitcast(FP8X4), scales=scales[:], in_=grouped[:].rearrange("p q j -> p (q j)")
+                out=q_codes[:].bitcast(FP8X4), scales=q_scales[:], in_=q_grouped[:].rearrange("p q t -> p (q t)")
             )
-            bank = ps.tile([Q, I], F32, name=name + "_bank", tag=name + "_bank")
+            score_bank = ps.tile([Q, I], F32, name=name + "_bank", tag=name + "_bank")
             nc.tensor.matmul_mx(
-                out=bank[:],
-                lhsT=codes[:].bitcast(FP8X4),
-                lhsT_scale=scales[:],
+                out=score_bank[:],
+                lhsT=q_codes[:].bitcast(FP8X4),
+                lhsT_scale=q_scales[:],
                 rhs=picked_words[:].bitcast(FP4X4),
                 rhs_scale=picked_bytes[:],
                 start=True,
                 stop=True,
             )
-            scores.append(bank)
+            scores.append(score_bank)
         a_ps, ta_ps = scores
 
         os_ps = ps.tile([P, PACK, P], F32, name="os_ps", tag="os_ps")
         for t in range(PACK):
-            nc.tensor.transpose(os_ps[:, t, :], os_cols[:, t : t + 1].to_broadcast([P, P]), ident[:])
+            nc.tensor.transpose(os_ps[:, t, :], one(os_cols, t).to_broadcast([P, P]), ident[:])
 
         by_r = sb.tile([P, 5], F32, name="by_r", tag="dq_raw")
-        nc.scalar.activation(by_r[:, 2:3], sharp_col[:], ACT.Copy, scale=-1.0)
-        nc.scalar.activation(by_r[:, 0:1], sharp_col[:], ACT.Copy)
-        nc.scalar.activation(by_r[:, 3:4], ones[:], ACT.Copy, scale=float(I))
-
-        def col(name):
-            return sb.tile([P, 1], F32, name=name)
-
-        def turn(rows, bank, grouped):
-            for n, tile in enumerate(rows):
-                words = tile[:].bitcast(F32)
-                for u in range(2):
-                    nc.tensor.transpose(bank[:, n, u, :], words[:, u::2], ident[:])
-            nc.scalar.copy(
-                grouped.bitcast(F32).rearrange("p (n x u) -> p n x u", n=len(rows), u=2),
-                bank[:].rearrange("p n u x -> p n x u"),
-            )
+        nc.scalar.activation(one(by_r, NEG_SHARP), sharp_col[:], ACT.Copy, scale=-1.0)
+        nc.scalar.activation(one(by_r, SHARP), sharp_col[:], ACT.Copy)
+        nc.scalar.activation(one(by_r, SLOTS), ones[:], ACT.Copy, scale=float(I))
 
         def gather_values(j):
-            picked = sb.tile([P, I], BF16, name="picked_vals%d" % j)
-            nc.vector.tensor_copy(picked[:], val_rows[j][:].indirect(offsets[:]))
-            return picked
+            listed = sb.tile([P, I], BF16, name="picked_vals%d" % j)
+            nc.vector.tensor_copy(listed[:], val_rows[j][:].indirect(offsets[:]))
+            return listed
 
-        junk_v = sb.tile([Q, I], BF16, name="junk_v")
-        nc.vector.tensor_scalar(junk_v[:], a_ps[:], by_r[:, 2:3], None, ALU.mult, ALU.min, accum_out=by_r[:, 1:2])
+        def turn(tiles, bank, grouped):
+            for n, tile in enumerate(tiles):
+                pairs = tile[:].bitcast(F32)
+                for h in range(2):
+                    nc.tensor.transpose(bank[:, n, h, :], pairs[:, h::2], ident[:])
+            nc.scalar.copy(
+                grouped.bitcast(F32).rearrange("p (n x h) -> p n x h", n=len(tiles), h=2),
+                bank[:].rearrange("p n h x -> p n x h"),
+            )
+
+        max_terms = sb.tile([Q, I], BF16, name="max_terms")
+        nc.vector.tensor_scalar(
+            max_terms[:], a_ps[:], one(by_r, NEG_SHARP), None, ALU.mult, ALU.min, accum_out=one(by_r, NEG_MAX)
+        )
         picked = [gather_values(0)]
-        a_sb = sb.tile([Q, I], F32, name="a_sb")
-        neg_mean = col("neg_mean")
-        nc.scalar.activation(a_sb[:], a_ps[:], ACT.Identity, scale=-1.0 / I, accum_out=neg_mean[:])
-        mean_n = col("mean_n")
-        nc.scalar.activation(mean_n[:], neg_mean[:], ACT.Copy, scale=1.0 / I)
-        junk_s = sb.tile([Q, I], BF16, name="junk_s")
-        sum_sq = col("sum_sq")
-        nc.scalar.activation(junk_s[:], a_ps[:], ACT.Square, bias=neg_mean[:], accum_out=sum_sq[:])
-        var_eps = col("var_eps")
-        nc.scalar.activation(var_eps[:], sum_sq[:], ACT.Copy, scale=1.0 / I, bias=EPS)
-        r = col("r")
+        a_scaled = sb.tile([Q, I], F32, name="a_scaled")
+        neg_mean = column("neg_mean")
+        nc.scalar.activation(a_scaled[:], a_ps[:], ACT.Identity, scale=-1.0 / I, accum_out=neg_mean[:])
+        square_terms = sb.tile([Q, I], BF16, name="square_terms")
+        sum_squares = column("sum_squares")
+        nc.scalar.activation(square_terms[:], a_ps[:], ACT.Square, bias=neg_mean[:], accum_out=sum_squares[:])
+        scaled_mean = column("scaled_mean")
+        nc.scalar.activation(scaled_mean[:], neg_mean[:], ACT.Copy, scale=1.0 / I)
+        var_eps = column("var_eps")
+        nc.scalar.activation(var_eps[:], sum_squares[:], ACT.Copy, scale=1.0 / I, bias=EPS)
+        r = column("r")
         nc.gpsimd.tensor_tensor(r[:], var_eps[:], minus_half[:], ALU.pow)
 
-        junk_c = sb.tile([Q, I], BF16, name="junk_c")
+        cov_terms = sb.tile([Q, I], BF16, name="cov_terms")
         nc.vector.scalar_tensor_tensor(
-            junk_c[:], a_sb[:], mean_n[:], ta_ps[:], ALU.subtract, ALU.mult, accum_out=by_r[:, 4:5]
+            cov_terms[:], a_scaled[:], scaled_mean[:], ta_ps[:], ALU.subtract, ALU.mult, accum_out=one(by_r, NEG_COV)
         )
         picked.append(gather_values(1))
 
         times_r = sb.tile([P, 5], F32, name="times_r")
         nc.scalar.activation(times_r[:], by_r[:], ACT.Copy, scale=r[:])
-        slope = col("slope")
-        nc.scalar.activation(slope[:], times_r[:, 4:5], ACT.Copy, scale=times_r[:, 3:4])
+        slope = column("slope")
+        nc.scalar.activation(slope[:], one(times_r, NEG_COV), ACT.Copy, scale=one(times_r, SLOTS))
         p = sb.tile([Q, I], F32, name="p")
-        z = col("z")
-        nc.scalar.activation(p[:], a_ps[:], ACT.Exp, scale=times_r[:, 0:1], bias=times_r[:, 1:2], accum_out=z[:])
+        z = column("z")
+        nc.scalar.activation(
+            p[:], a_ps[:], ACT.Exp, scale=one(times_r, SHARP), bias=one(times_r, NEG_MAX), accum_out=z[:]
+        )
 
-        u = sb.tile([Q, I], F32, name="u", tag="val_rows1", align_bytes=64)
-        nc.vector.scalar_tensor_tensor(u[:], a_sb[:], slope[:], ta_ps[:], ALU.mult, ALU.subtract)
-        rz = col("rz")
-        nc.vector.reciprocal(rz[:], z[:])
-        cz = col("cz")
-        nc.scalar.activation(cz[:], times_r[:, 2:3], ACT.Copy, scale=rz[:])
-        u_sum = col("u_sum")
-        junk_u = sb.tile([Q, I], BF16, name="junk_u")
-        nc.vector.scalar_tensor_tensor(junk_u[:], u[:], 1.0, p[:], ALU.mult, ALU.mult, accum_out=u_sum[:])
-        u_mean = col("u_mean")
-        nc.scalar.activation(u_mean[:], u_sum[:], ACT.Copy, scale=rz[:])
-        x = sb.tile([Q, I], F32, name="x")
+        neg_u = sb.tile([Q, I], F32, name="neg_u")
+        nc.vector.scalar_tensor_tensor(neg_u[:], a_scaled[:], slope[:], ta_ps[:], ALU.mult, ALU.subtract)
+        inv_z = column("inv_z")
+        nc.vector.reciprocal(inv_z[:], z[:])
+        neg_c_by_z = column("neg_c_by_z")
+        nc.scalar.activation(neg_c_by_z[:], one(times_r, NEG_SHARP), ACT.Copy, scale=inv_z[:])
+        neg_u_sum = column("neg_u_sum")
+        mean_terms = sb.tile([Q, I], BF16, name="mean_terms")
+        nc.vector.scalar_tensor_tensor(mean_terms[:], neg_u[:], 1.0, p[:], ALU.mult, ALU.mult, accum_out=neg_u_sum[:])
+        neg_u_mean = column("neg_u_mean")
+        nc.scalar.activation(neg_u_mean[:], neg_u_sum[:], ACT.Copy, scale=inv_z[:])
+        factor = sb.tile([Q, I], F32, name="factor")
         nc.vector.scalar_tensor_tensor(
-            x[:].rearrange("q (p t) -> q p t", t=PACK),
-            p[:].rearrange("q (p t) -> q p t", t=PACK),
-            cz[:],
-            os_ps[:].rearrange("q t p -> q p t"),
+            factor[:].rearrange("q (s t) -> q s t", t=PACK),
+            p[:].rearrange("q (s t) -> q s t", t=PACK),
+            neg_c_by_z[:],
+            os_ps[:].rearrange("q t s -> q s t"),
             ALU.mult,
             ALU.mult,
         )
-        w = sb.tile([Q, I], BF16, name="w")
-        nc.vector.scalar_tensor_tensor(w[:], u[:], u_mean[:], x[:], ALU.subtract, ALU.mult)
+        wo1 = sb.tile([Q, I], BF16, name="wo1")
+        nc.vector.scalar_tensor_tensor(wo1[:], neg_u[:], neg_u_mean[:], factor[:], ALU.subtract, ALU.mult)
         picked.append(gather_values(2))
         picked.append(gather_values(3))
 
-        grouped = sb.tile([P, 5 * I], BF16, name="grouped", align_bytes=64)
+        grouped = sb.tile([P, (VALUE_TILES + 1) * I], BF16, name="grouped", align_bytes=MX_ALIGN)
         turn(picked[0:2], ps.tile([P, 2, 2, P], F32, name="turned01", tag="q_bank"), grouped[:, 0 : 2 * I])
-        turn([w], ps.tile([P, 1, 2, P], F32, name="turned_w"), grouped[:, 4 * I :])
+        turn([wo1], ps.tile([P, 1, 2, P], F32, name="turned_w"), grouped[:, WEIGHTS * I :])
         turn(picked[2:3], ps.tile([P, 1, 2, P], F32, name="turned2"), grouped[:, 2 * I : 3 * I])
         turn(picked[3:4], ps.tile([P, 1, 2, P], F32, name="turned3"), grouped[:, 3 * I : 4 * I])
 
-        codes = sb.tile([P, 5 * P], U32, name="codes", tag="val_rows3", align_bytes=64)
-        scales = sb.tile([P, 5 * P], U8, name="scales", align_bytes=64)
-        for lo, hi in ((4, 5), (0, 2), (2, 3), (3, 4)):
+        codes = sb.tile([P, (VALUE_TILES + 1) * P], U32, name="codes", tag="val_rows3", align_bytes=MX_ALIGN)
+        scales = sb.tile([P, (VALUE_TILES + 1) * P], U8, name="scales", align_bytes=MX_ALIGN)
+        value_groups = ((0, 2), (2, 3), (3, 4))
+        for lo, hi in ((WEIGHTS, WEIGHTS + 1),) + value_groups:
             nc.vector.quantize_mx(
                 out=codes[:, lo * P : hi * P].bitcast(FP8X4),
                 scales=scales[:, lo * P : hi * P],
                 in_=grouped[:, lo * I : hi * I],
             )
 
-        def product(bank, lo, hi):
+        bank_tags = ("out01", "os_ps", "out3")
+        copies = (nc.scalar.copy, nc.vector.tensor_copy, nc.vector.tensor_copy)
+        for (lo, hi), tag, copy in zip(value_groups, bank_tags, copies):
+            features = slice(lo * P, hi * P)
+            out_bank = ps.tile([Q, (hi - lo) * P], F32, name="out_bank%d" % lo, tag=tag)
             nc.tensor.matmul_mx(
-                out=bank,
-                lhsT=codes[:, 4 * P :].bitcast(FP8X4),
-                lhsT_scale=scales[:, 4 * P :],
-                rhs=codes[:, lo:hi].bitcast(FP8X4),
-                rhs_scale=scales[:, lo:hi],
+                out=out_bank[:],
+                lhsT=codes[:, WEIGHTS * P :].bitcast(FP8X4),
+                lhsT_scale=scales[:, WEIGHTS * P :],
+                rhs=codes[:, features].bitcast(FP8X4),
+                rhs_scale=scales[:, features],
                 start=True,
                 stop=True,
             )
-
-        for lo, hi, tag, copy in (
-            (0, 2 * P, "out01", nc.scalar.copy),
-            (2 * P, 3 * P, "os_ps", nc.vector.tensor_copy),
-            (3 * P, 4 * P, "out3", nc.vector.tensor_copy),
-        ):
-            bank = ps.tile([Q, hi - lo], F32, name="out_bank%d" % lo, tag=tag)
-            product(bank[:], lo, hi)
-            result = sb.tile([Q, hi - lo], F32, name="result%d" % lo)
-            copy(result[:], bank[:])
-            nc.sync.dma_start(out[:, lo:hi], result[:])
+            result = sb.tile([Q, (hi - lo) * P], F32, name="result%d" % lo)
+            copy(result[:], out_bank[:])
+            nc.sync.dma_start(out[:, features], result[:])

from contextlib import ExitStack

import concourse.mybir as mybir
from concourse.masks import make_identity

F32 = mybir.dt.float32
BF16 = mybir.dt.bfloat16
I32 = mybir.dt.int32
U32 = mybir.dt.uint32
U16 = mybir.dt.uint16
U8 = mybir.dt.uint8
FP8X4 = mybir.dt.float8_e4m3fn_x4
FP4X4 = mybir.dt.float4_e2m1fn_x4
ALU = mybir.AluOpType
ACT = mybir.ActivationFunctionType

D, E, T, I, Q = 512, 512, 2048, 512, 128
P = 128
PACK = 4
LIST_ROWS = 16
QUADRANT = 32
VALUE_TILES = E // P
MX_ALIGN = 64
EPS = 0.05
FLOPS = 2 * Q * I * (2 * D + E)

SHARP, NEG_MAX, NEG_SHARP, SLOTS, NEG_COV = range(5)
WEIGHTS = VALUE_TILES


def tile_attend_ttstandardised_kernel(tc, query, keys_words, keys_scales, sharp, dquery, slot_factor, vals, offs, out):
    nc = tc.nc
    with ExitStack() as ctx:
        sb = ctx.enter_context(tc.tile_pool(name="sb", bufs=1))
        ps = ctx.enter_context(tc.psum_pool(name="ps", bufs=1))

        def column(name):
            return sb.tile([P, 1], F32, name=name)

        def one(tile, n):
            return tile[:, n : n + 1]

        offsets = sb.tile([P, I // LIST_ROWS], U16, name="offsets")
        nc.sync.dma_start(offsets[:], offs)

        raw = [sb.tile([P, PACK, Q], F32, name=name, tag=name) for name in ("q_raw", "dq_raw")]

        key_bytes = sb.tile([P, T], U8, name="key_bytes")
        nc.vector.memset(key_bytes[:].bitcast(I32), 0)
        for quad in range(P // QUADRANT):
            nc.sync.dma_start(
                key_bytes[QUADRANT * quad : QUADRANT * quad + 4, :].bitcast(I32),
                keys_scales[0, 4 * quad : 4 * quad + 4, :].bitcast(I32),
            )
        key_words = sb.tile([P, T], U16, name="key_words")
        nc.sync.dma_start(key_words[:].bitcast(I32), keys_words[0].bitcast(I32))

        val_rows = [
            sb.tile([P, T], F32, name="val_rows%d" % j, tag="val_rows%d" % j, align_bytes=MX_ALIGN)
            for j in range(VALUE_TILES)
        ]
        nc.sync.dma_start(raw[0][:], query.rearrange("(p t) q -> p t q", t=PACK))
        nc.sync.dma_start(raw[1][:], dquery.rearrange("(p t) q -> p t q", t=PACK))
        for j in range(VALUE_TILES):
            nc.sync.dma_start(val_rows[j][:], vals[j * P : (j + 1) * P, :])

        sharp_col = column("sharp_col")
        nc.gpsimd.dma_start(sharp_col[:], sharp)
        os_cols = sb.tile([P, PACK], F32, name="os_cols")
        nc.gpsimd.dma_start(os_cols[:], slot_factor.rearrange("o (p t) -> (o p) t", t=PACK))

        ones = column("ones")
        nc.gpsimd.memset(ones[:], 1.0)
        minus_half = column("minus_half")
        nc.scalar.activation(minus_half[:], ones[:], ACT.Copy, scale=-0.5)
        ident = sb.tile([P, P], F32, name="ident")
        make_identity(nc, ident[:])

        picked_bytes = sb.tile([P, I], U8, name="picked_bytes", align_bytes=MX_ALIGN)
        nc.vector.tensor_copy(picked_bytes[:], key_bytes[:].indirect(offsets[:]))
        picked_words = sb.tile([P, I], U16, name="picked_words", align_bytes=MX_ALIGN)
        nc.vector.tensor_copy(picked_words[:], key_words[:].indirect(offsets[:]))

        scores = []
        for name, rows in zip(("q", "dq"), raw):
            q_grouped = sb.tile([P, Q, PACK], BF16, name=name + "_grouped", align_bytes=MX_ALIGN)
            nc.scalar.activation(q_grouped[:], rows[:].rearrange("p t q -> p q t"), ACT.Copy)
            q_codes = sb.tile([P, Q], U32, name=name + "_codes", align_bytes=MX_ALIGN)
            q_scales = sb.tile([P, Q], U8, name=name + "_scales", align_bytes=MX_ALIGN)
            nc.vector.quantize_mx(
                out=q_codes[:].bitcast(FP8X4), scales=q_scales[:], in_=q_grouped[:].rearrange("p q t -> p (q t)")
            )
            score_bank = ps.tile([Q, I], F32, name=name + "_bank", tag=name + "_bank")
            nc.tensor.matmul_mx(
                out=score_bank[:],
                lhsT=q_codes[:].bitcast(FP8X4),
                lhsT_scale=q_scales[:],
                rhs=picked_words[:].bitcast(FP4X4),
                rhs_scale=picked_bytes[:],
                start=True,
                stop=True,
            )
            scores.append(score_bank)
        a_ps, ta_ps = scores

        os_ps = ps.tile([P, PACK, P], F32, name="os_ps", tag="os_ps")
        for t in range(PACK):
            nc.tensor.transpose(os_ps[:, t, :], one(os_cols, t).to_broadcast([P, P]), ident[:])

        by_r = sb.tile([P, 5], F32, name="by_r", tag="dq_raw")
        nc.scalar.activation(one(by_r, NEG_SHARP), sharp_col[:], ACT.Copy, scale=-1.0)
        nc.scalar.activation(one(by_r, SHARP), sharp_col[:], ACT.Copy)
        nc.scalar.activation(one(by_r, SLOTS), ones[:], ACT.Copy, scale=float(I))

        def gather_values(j):
            listed = sb.tile([P, I], BF16, name="picked_vals%d" % j)
            nc.vector.tensor_copy(listed[:], val_rows[j][:].indirect(offsets[:]))
            return listed

        def turn(tiles, bank, grouped):
            for n, tile in enumerate(tiles):
                pairs = tile[:].bitcast(F32)
                for h in range(2):
                    nc.tensor.transpose(bank[:, n, h, :], pairs[:, h::2], ident[:])
            nc.scalar.copy(
                grouped.bitcast(F32).rearrange("p (n x h) -> p n x h", n=len(tiles), h=2),
                bank[:].rearrange("p n h x -> p n x h"),
            )

        max_terms = sb.tile([Q, I], BF16, name="max_terms")
        nc.vector.tensor_scalar(
            max_terms[:], a_ps[:], one(by_r, NEG_SHARP), None, ALU.mult, ALU.min, accum_out=one(by_r, NEG_MAX)
        )
        picked = [gather_values(0)]
        a_scaled = sb.tile([Q, I], F32, name="a_scaled")
        neg_mean = column("neg_mean")
        nc.scalar.activation(a_scaled[:], a_ps[:], ACT.Identity, scale=-1.0 / I, accum_out=neg_mean[:])
        square_terms = sb.tile([Q, I], BF16, name="square_terms")
        sum_squares = column("sum_squares")
        nc.scalar.activation(square_terms[:], a_ps[:], ACT.Square, bias=neg_mean[:], accum_out=sum_squares[:])
        scaled_mean = column("scaled_mean")
        nc.scalar.activation(scaled_mean[:], neg_mean[:], ACT.Copy, scale=1.0 / I)
        var_eps = column("var_eps")
        nc.scalar.activation(var_eps[:], sum_squares[:], ACT.Copy, scale=1.0 / I, bias=EPS)
        r = column("r")
        nc.gpsimd.tensor_tensor(r[:], var_eps[:], minus_half[:], ALU.pow)

        cov_terms = sb.tile([Q, I], BF16, name="cov_terms")
        nc.vector.scalar_tensor_tensor(
            cov_terms[:], a_scaled[:], scaled_mean[:], ta_ps[:], ALU.subtract, ALU.mult, accum_out=one(by_r, NEG_COV)
        )
        picked.append(gather_values(1))

        times_r = sb.tile([P, 5], F32, name="times_r")
        nc.scalar.activation(times_r[:], by_r[:], ACT.Copy, scale=r[:])
        slope = column("slope")
        nc.scalar.activation(slope[:], one(times_r, NEG_COV), ACT.Copy, scale=one(times_r, SLOTS))
        p = sb.tile([Q, I], F32, name="p")
        z = column("z")
        nc.scalar.activation(
            p[:], a_ps[:], ACT.Exp, scale=one(times_r, SHARP), bias=one(times_r, NEG_MAX), accum_out=z[:]
        )

        neg_u = sb.tile([Q, I], F32, name="neg_u")
        nc.vector.scalar_tensor_tensor(neg_u[:], a_scaled[:], slope[:], ta_ps[:], ALU.mult, ALU.subtract)
        inv_z = column("inv_z")
        nc.vector.reciprocal(inv_z[:], z[:])
        neg_c_by_z = column("neg_c_by_z")
        nc.scalar.activation(neg_c_by_z[:], one(times_r, NEG_SHARP), ACT.Copy, scale=inv_z[:])
        neg_u_sum = column("neg_u_sum")
        mean_terms = sb.tile([Q, I], BF16, name="mean_terms")
        nc.vector.scalar_tensor_tensor(mean_terms[:], neg_u[:], 1.0, p[:], ALU.mult, ALU.mult, accum_out=neg_u_sum[:])
        neg_u_mean = column("neg_u_mean")
        nc.scalar.activation(neg_u_mean[:], neg_u_sum[:], ACT.Copy, scale=inv_z[:])
        factor = sb.tile([Q, I], F32, name="factor")
        nc.vector.scalar_tensor_tensor(
            factor[:].rearrange("q (s t) -> q s t", t=PACK),
            p[:].rearrange("q (s t) -> q s t", t=PACK),
            neg_c_by_z[:],
            os_ps[:].rearrange("q t s -> q s t"),
            ALU.mult,
            ALU.mult,
        )
        wo1 = sb.tile([Q, I], BF16, name="wo1")
        nc.vector.scalar_tensor_tensor(wo1[:], neg_u[:], neg_u_mean[:], factor[:], ALU.subtract, ALU.mult)
        picked.append(gather_values(2))
        picked.append(gather_values(3))

        grouped = sb.tile([P, (VALUE_TILES + 1) * I], BF16, name="grouped", align_bytes=MX_ALIGN)
        turn(picked[0:2], ps.tile([P, 2, 2, P], F32, name="turned01", tag="q_bank"), grouped[:, 0 : 2 * I])
        turn([wo1], ps.tile([P, 1, 2, P], F32, name="turned_w"), grouped[:, WEIGHTS * I :])
        turn(picked[2:3], ps.tile([P, 1, 2, P], F32, name="turned2"), grouped[:, 2 * I : 3 * I])
        turn(picked[3:4], ps.tile([P, 1, 2, P], F32, name="turned3"), grouped[:, 3 * I : 4 * I])

        codes = sb.tile([P, (VALUE_TILES + 1) * P], U32, name="codes", tag="val_rows3", align_bytes=MX_ALIGN)
        scales = sb.tile([P, (VALUE_TILES + 1) * P], U8, name="scales", align_bytes=MX_ALIGN)
        value_groups = ((0, 2), (2, 3), (3, 4))
        for lo, hi in ((WEIGHTS, WEIGHTS + 1),) + value_groups:
            nc.vector.quantize_mx(
                out=codes[:, lo * P : hi * P].bitcast(FP8X4),
                scales=scales[:, lo * P : hi * P],
                in_=grouped[:, lo * I : hi * I],
            )

        bank_tags = ("out01", "os_ps", "out3")
        copies = (nc.scalar.copy, nc.vector.tensor_copy, nc.vector.tensor_copy)
        for (lo, hi), tag, copy in zip(value_groups, bank_tags, copies):
            features = slice(lo * P, hi * P)
            out_bank = ps.tile([Q, (hi - lo) * P], F32, name="out_bank%d" % lo, tag=tag)
            nc.tensor.matmul_mx(
                out=out_bank[:],
                lhsT=codes[:, WEIGHTS * P :].bitcast(FP8X4),
                lhsT_scale=scales[:, WEIGHTS * P :],
                rhs=codes[:, features].bitcast(FP8X4),
                rhs_scale=scales[:, features],
                start=True,
                stop=True,
            )
            result = sb.tile([Q, (hi - lo) * P], F32, name="result%d" % lo)
            copy(result[:], out_bank[:])
            nc.sync.dma_start(out[:, features], result[:])
